import numpy as np
CORES = [3,11,19,27,131,139,147,155,259,267,275,283,387,395,403,411]
N = 16
def setup_inputs(rng):
    return {"x": rng.standard_normal((N, 128, 32), dtype=np.float32)}
def reference(x):
    s = x.min(axis=0)
    return {"y": np.broadcast_to(s, (N,) + s.shape)}

@@ -1,0 +1,52 @@
+from concourse.bass import DstId, RemoteDMATransfer
+
+SCRATCH = {
+    "xs": ("sbuf", [128, 32], "float32"),
+    "r1": ("sbuf", [128, 96], "float32"),
+    "r2": ("sbuf", [128, 96], "float32"),
+    "out": ("sbuf", [128, 32], "float32"),
+}
+SEMAPHORES = ["ld", "a1", "a2", "a3", "sent", "st"]
+MIN = 3
+PLANE = [(0, 2), (1, 0), (1, 2)]
+CROSS = [(0, 1), (1, 0), (1, 1)]
+
+
+def rank_program(g, core, T, topo):
+    if T.rank_of(core) is None:
+        return
+    h, c = topo.host(core), topo.chip(core)
+
+    def did(p):
+        rid, pid = topo.addr(p[0] * 128 + p[1] * 8 + 3, core)
+        return DstId(rid=rid, pnc=pid)
+
+    plane = [(h ^ a, c ^ b) for a, b in PLANE]
+    cross = [((3 - h) if a else h, c ^ b) for a, b in CROSS]
+    r1 = [T.r1[:, 32 * k:32 * k + 32] for k in range(3)]
+    r2 = [T.r2[:, 32 * k:32 * k + 32] for k in range(3)]
+
+    g.dma_start(T.xs[:], T.x[:]).then_inc(T.sem.ld, 16)
+    g.wait_ge(T.sem.ld, 16)
+
+    g.remote_dma_fused(
+        [RemoteDMATransfer(dst_ids=[did(p) for p in plane], dma_engine_mask=0xFF, remote_sem=T.sem.a1,
+                           srcs=[T.xs[:]], dsts=r1)],
+        local_sem=T.sem.sent)
+    g.wait_ge(T.sem.a1, 24)
+
+    g.remote_dma_fused(
+        [RemoteDMATransfer(dst_ids=[did(p) for p in cross], dma_engine_mask=0xFF, remote_sem=T.sem.a2,
+                           srcs=[T.xs[:]] + r1, dsts=r2, alu_op=MIN)],
+        local_sem=T.sem.sent)
+    g.wait_ge(T.sem.a2, 24)
+
+    g.remote_dma_fused(
+        [RemoteDMATransfer(dst_ids=[did((h, c ^ 1))], dma_engine_mask=0xFF, remote_sem=T.sem.a3,
+                           srcs=[T.xs[:]] + r1 + r2, dsts=[T.out[:]], alu_op=MIN)],
+        local_sem=T.sem.sent)
+    g.wait_ge(T.sem.a3, 8)
+
+    g.dma_start(T.y[:], T.out[:]).then_inc(T.sem.st, 16)
+    g.wait_ge(T.sem.sent, 24)
+    g.wait_ge(T.sem.st, 16)

@@ -1,10 +1,12 @@
 from concourse.bass import DstId, RemoteDMATransfer
 
+NP = 4
+W = 32 // NP
 SCRATCH = {
-    "xs": ("sbuf", [128, 32], "float32"),
-    "r1": ("sbuf", [128, 96], "float32"),
-    "r2": ("sbuf", [128, 96], "float32"),
-    "out": ("sbuf", [128, 32], "float32"),
+    "xs": ("dram", [NP, 128, W], "float32"),
+    "r1": ("dram", [3, 128, W], "float32"),
+    "r2": ("dram", [3, 128, W], "float32"),
+    "out": ("dram", [NP, 128, W], "float32"),
 }
 SEMAPHORES = ["ld", "a1", "a2", "a3", "sent", "st"]
 MIN = 3
@@ -17,36 +19,43 @@ def rank_program(g, core, T, topo):
         return
     h, c = topo.host(core), topo.chip(core)
 
-    def did(p):
-        rid, pid = topo.addr(p[0] * 128 + p[1] * 8 + 3, core)
+    def rk(hh, cc):
+        return hh * 128 + cc * 8 + 3
+
+    def piece(hh, cc):
+        return 2 * (1 if hh in (1, 2) else 0) + (cc >> 1)
+
+    def did(d):
+        rid, pid = topo.addr(d, core)
         return DstId(rid=rid, pnc=pid)
 
     plane = [(h ^ a, c ^ b) for a, b in PLANE]
     cross = [((3 - h) if a else h, c ^ b) for a, b in CROSS]
-    r1 = [T.r1[:, 32 * k:32 * k + 32] for k in range(3)]
-    r2 = [T.r2[:, 32 * k:32 * k + 32] for k in range(3)]
+    me = piece(h, c)
 
     g.dma_start(T.xs[:], T.x[:]).then_inc(T.sem.ld, 16)
     g.wait_ge(T.sem.ld, 16)
 
     g.remote_dma_fused(
-        [RemoteDMATransfer(dst_ids=[did(p) for p in plane], dma_engine_mask=0xFF, remote_sem=T.sem.a1,
-                           srcs=[T.xs[:]], dsts=r1)],
+        [RemoteDMATransfer(dst_ids=[did(rk(*p))], dma_engine_mask=0x3 << (2 * k), remote_sem=T.sem.a1,
+                           src=T.xs[piece(*p)], dst=T.r1[k]) for k, p in enumerate(plane)],
         local_sem=T.sem.sent)
-    g.wait_ge(T.sem.a1, 24)
+    g.wait_ge(T.sem.a1, 6)
 
+    part = [T.xs[me], T.r1[0], T.r1[1], T.r1[2]]
     g.remote_dma_fused(
-        [RemoteDMATransfer(dst_ids=[did(p) for p in cross], dma_engine_mask=0xFF, remote_sem=T.sem.a2,
-                           srcs=[T.xs[:]] + r1, dsts=r2, alu_op=MIN)],
+        [RemoteDMATransfer(dst_ids=[did(rk(*p)) for p in cross], dma_engine_mask=0xFF, remote_sem=T.sem.a2,
+                           srcs=part, dsts=[T.r2[k] for k in range(3)], alu_op=MIN)],
         local_sem=T.sem.sent)
     g.wait_ge(T.sem.a2, 24)
 
+    to = plane + [(h, c ^ 1)]
     g.remote_dma_fused(
-        [RemoteDMATransfer(dst_ids=[did((h, c ^ 1))], dma_engine_mask=0xFF, remote_sem=T.sem.a3,
-                           srcs=[T.xs[:]] + r1 + r2, dsts=[T.out[:]], alu_op=MIN)],
+        [RemoteDMATransfer(dst_ids=[did(rk(*p)) for p in to], dma_engine_mask=0xFF, remote_sem=T.sem.a3,
+                           srcs=part + [T.r2[0], T.r2[1], T.r2[2]], dsts=[T.out[me]] * 4, alu_op=MIN)],
         local_sem=T.sem.sent)
-    g.wait_ge(T.sem.a3, 8)
+    g.wait_ge(T.sem.a3, 32)
 
     g.dma_start(T.y[:], T.out[:]).then_inc(T.sem.st, 16)
-    g.wait_ge(T.sem.sent, 24)
+    g.wait_ge(T.sem.sent, 6 + 8 + 8)
     g.wait_ge(T.sem.st, 16)

@@ -10,8 +10,8 @@ SCRATCH = {
 }
 SEMAPHORES = ["ld", "a1", "a2", "a3", "sent", "st"]
 MIN = 3
-PLANE = [(0, 2), (1, 0), (1, 2)]
-CROSS = [(0, 1), (1, 0), (1, 1)]
+PLANE = [(1, 2), (1, 0), (0, 2)]
+CROSS = [(1, 1), (1, 0), (0, 1)]
 
 
 def rank_program(g, core, T, topo):

@@ -1,61 +1,70 @@
 from concourse.bass import DstId, RemoteDMATransfer
 
-NP = 4
-W = 32 // NP
+W = 4
 SCRATCH = {
-    "xs": ("dram", [NP, 128, W], "float32"),
-    "r1": ("dram", [3, 128, W], "float32"),
+    "xs": ("dram", [8, 128, W], "float32"),
+    "r1": ("dram", [4, 128, W], "float32"),
     "r2": ("dram", [3, 128, W], "float32"),
-    "out": ("dram", [NP, 128, W], "float32"),
+    "out": ("dram", [8, 128, W], "float32"),
 }
 SEMAPHORES = ["ld", "a1", "a2", "a3", "sent", "st"]
 MIN = 3
 PLANE = [(1, 2), (1, 0), (0, 2)]
 CROSS = [(1, 1), (1, 0), (0, 1)]
+ROLE_CORE = (3, 7)
 
 
 def rank_program(g, core, T, topo):
-    if T.rank_of(core) is None:
-        return
     h, c = topo.host(core), topo.chip(core)
+    if c > 3 or core % 8 not in ROLE_CORE:
+        return
+    role = ROLE_CORE.index(core % 8)
 
-    def rk(hh, cc):
-        return hh * 128 + cc * 8 + 3
-
-    def piece(hh, cc):
-        return 2 * (1 if hh in (1, 2) else 0) + (cc >> 1)
-
-    def did(d):
-        rid, pid = topo.addr(d, core)
+    def did(p, r):
+        rid, pid = topo.addr(p[0] * 128 + p[1] * 8 + ROLE_CORE[r], core)
         return DstId(rid=rid, pnc=pid)
+
+    def piece(p):
+        return 2 * (1 if p[0] in (1, 2) else 0) + (p[1] >> 1)
 
     plane = [(h ^ a, c ^ b) for a, b in PLANE]
     cross = [((3 - h) if a else h, c ^ b) for a, b in CROSS]
-    me = piece(h, c)
+    me = 2 * piece((h, c)) + role
+    sent = 16
 
-    g.dma_start(T.xs[:], T.x[:]).then_inc(T.sem.ld, 16)
-    g.wait_ge(T.sem.ld, 16)
+    if role == 0:
+        g.dma_start(T.xs[:], T.x[:]).then_inc(T.sem.ld, 16)
+        g.wait_ge(T.sem.ld, 16)
+        g.remote_dma_fused(
+            [RemoteDMATransfer(dst_ids=[did(p, r)], dma_engine_mask=1 << (2 * k + r), remote_sem=T.sem.a1,
+                               src=T.xs[2 * piece(p) + r], dst=T.r1[k])
+             for k, p in enumerate(plane) for r in range(2)]
+            + [RemoteDMATransfer(dst_ids=[did((h, c), 1)], dma_engine_mask=0xFF00, remote_sem=T.sem.a1,
+                                 src=T.xs[me + 1], dst=T.r1[3])],
+            local_sem=T.sem.sent)
+        sent += 6 + 8
+        g.wait_ge(T.sem.a1, 3)
+        part = [T.xs[me], T.r1[0], T.r1[1], T.r1[2]]
+    else:
+        g.wait_ge(T.sem.a1, 3 + 8)
+        part = [T.r1[3], T.r1[0], T.r1[1], T.r1[2]]
 
     g.remote_dma_fused(
-        [RemoteDMATransfer(dst_ids=[did(rk(*p))], dma_engine_mask=0x3 << (2 * k), remote_sem=T.sem.a1,
-                           src=T.xs[piece(*p)], dst=T.r1[k]) for k, p in enumerate(plane)],
-        local_sem=T.sem.sent)
-    g.wait_ge(T.sem.a1, 6)
-
-    part = [T.xs[me], T.r1[0], T.r1[1], T.r1[2]]
-    g.remote_dma_fused(
-        [RemoteDMATransfer(dst_ids=[did(rk(*p)) for p in cross], dma_engine_mask=0xFF, remote_sem=T.sem.a2,
+        [RemoteDMATransfer(dst_ids=[did(p, role) for p in cross], dma_engine_mask=0xFF, remote_sem=T.sem.a2,
                            srcs=part, dsts=[T.r2[k] for k in range(3)], alu_op=MIN)],
         local_sem=T.sem.sent)
     g.wait_ge(T.sem.a2, 24)
 
-    to = plane + [(h, c ^ 1)]
+    to = plane + [(h, c ^ 1) if role == 0 else (h, c)]
     g.remote_dma_fused(
-        [RemoteDMATransfer(dst_ids=[did(rk(*p)) for p in to], dma_engine_mask=0xFF, remote_sem=T.sem.a3,
+        [RemoteDMATransfer(dst_ids=[did(p, 0) for p in to], dma_engine_mask=0xFF, remote_sem=T.sem.a3,
                            srcs=part + [T.r2[0], T.r2[1], T.r2[2]], dsts=[T.out[me]] * 4, alu_op=MIN)],
         local_sem=T.sem.sent)
-    g.wait_ge(T.sem.a3, 32)
 
-    g.dma_start(T.y[:], T.out[:]).then_inc(T.sem.st, 16)
-    g.wait_ge(T.sem.sent, 6 + 8 + 8)
-    g.wait_ge(T.sem.st, 16)
+    if role == 0:
+        g.wait_ge(T.sem.a3, 64)
+        g.dma_start(T.y[:], T.out[:]).then_inc(T.sem.st, 16)
+        g.wait_ge(T.sem.sent, sent)
+        g.wait_ge(T.sem.st, 16)
+    else:
+        g.wait_ge(T.sem.sent, sent)

@@ -39,14 +39,14 @@ def rank_program(g, core, T, topo):
             [RemoteDMATransfer(dst_ids=[did(p, r)], dma_engine_mask=1 << (2 * k + r), remote_sem=T.sem.a1,
                                src=T.xs[2 * piece(p) + r], dst=T.r1[k])
              for k, p in enumerate(plane) for r in range(2)]
-            + [RemoteDMATransfer(dst_ids=[did((h, c), 1)], dma_engine_mask=0xFF00, remote_sem=T.sem.a1,
+            + [RemoteDMATransfer(dst_ids=[did((h, c), 1)], dma_engine_mask=1 << 6, remote_sem=T.sem.a1,
                                  src=T.xs[me + 1], dst=T.r1[3])],
             local_sem=T.sem.sent)
-        sent += 6 + 8
+        sent += 7
         g.wait_ge(T.sem.a1, 3)
         part = [T.xs[me], T.r1[0], T.r1[1], T.r1[2]]
     else:
-        g.wait_ge(T.sem.a1, 3 + 8)
+        g.wait_ge(T.sem.a1, 4)
         part = [T.r1[3], T.r1[0], T.r1[1], T.r1[2]]
 
     g.remote_dma_fused(

from concourse.bass import DstId, RemoteDMATransfer

W = 4
SCRATCH = {
    "xs": ("dram", [8, 128, W], "float32"),
    "r1": ("dram", [4, 128, W], "float32"),
    "r2": ("dram", [3, 128, W], "float32"),
    "out": ("dram", [8, 128, W], "float32"),
}
SEMAPHORES = ["ld", "a1", "a2", "a3", "sent", "st"]
MIN = 3
PLANE = [(1, 2), (1, 0), (0, 2)]
CROSS = [(1, 1), (1, 0), (0, 1)]
ROLE_CORE = (3, 7)


def rank_program(g, core, T, topo):
    h, c = topo.host(core), topo.chip(core)
    if c > 3 or core % 8 not in ROLE_CORE:
        return
    role = ROLE_CORE.index(core % 8)

    def did(p, r):
        rid, pid = topo.addr(p[0] * 128 + p[1] * 8 + ROLE_CORE[r], core)
        return DstId(rid=rid, pnc=pid)

    def piece(p):
        return 2 * (1 if p[0] in (1, 2) else 0) + (p[1] >> 1)

    plane = [(h ^ a, c ^ b) for a, b in PLANE]
    cross = [((3 - h) if a else h, c ^ b) for a, b in CROSS]
    me = 2 * piece((h, c)) + role
    sent = 16

    if role == 0:
        g.dma_start(T.xs[:], T.x[:]).then_inc(T.sem.ld, 16)
        g.wait_ge(T.sem.ld, 16)
        g.remote_dma_fused(
            [RemoteDMATransfer(dst_ids=[did(p, r)], dma_engine_mask=1 << (2 * k + r), remote_sem=T.sem.a1,
                               src=T.xs[2 * piece(p) + r], dst=T.r1[k])
             for k, p in enumerate(plane) for r in range(2)]
            + [RemoteDMATransfer(dst_ids=[did((h, c), 1)], dma_engine_mask=1 << 6, remote_sem=T.sem.a1,
                                 src=T.xs[me + 1], dst=T.r1[3])],
            local_sem=T.sem.sent)
        sent += 7
        g.wait_ge(T.sem.a1, 3)
        part = [T.xs[me], T.r1[0], T.r1[1], T.r1[2]]
    else:
        g.wait_ge(T.sem.a1, 4)
        part = [T.r1[3], T.r1[0], T.r1[1], T.r1[2]]

    g.remote_dma_fused(
        [RemoteDMATransfer(dst_ids=[did(p, role) for p in cross], dma_engine_mask=0xFF, remote_sem=T.sem.a2,
                           srcs=part, dsts=[T.r2[k] for k in range(3)], alu_op=MIN)],
        local_sem=T.sem.sent)
    g.wait_ge(T.sem.a2, 24)

    to = plane + [(h, c ^ 1) if role == 0 else (h, c)]
    g.remote_dma_fused(
        [RemoteDMATransfer(dst_ids=[did(p, 0) for p in to], dma_engine_mask=0xFF, remote_sem=T.sem.a3,
                           srcs=part + [T.r2[0], T.r2[1], T.r2[2]], dsts=[T.out[me]] * 4, alu_op=MIN)],
        local_sem=T.sem.sent)

    if role == 0:
        g.wait_ge(T.sem.a3, 64)
        g.dma_start(T.y[:], T.out[:]).then_inc(T.sem.st, 16)
        g.wait_ge(T.sem.sent, sent)
        g.wait_ge(T.sem.st, 16)
    else:
        g.wait_ge(T.sem.sent, sent)
